import numpy as np
import ml_dtypes


def mxq(x, axis, fmt="e4m3"):
    dtype, down = {"e4m3": (ml_dtypes.float8_e4m3fn, 7), "e5m2": (ml_dtypes.float8_e5m2, 14)}[fmt]
    v = np.moveaxis(np.asarray(x, np.float32).astype(ml_dtypes.bfloat16).astype(np.float64), axis, -1)
    blocks = v.reshape(v.shape[:-1] + (-1, 32))
    amax = np.abs(blocks).max(-1, keepdims=True)
    byte = np.maximum(np.where(amax > 0, np.frexp(amax)[1] - 1 + 127, 0) - down, 1)
    scale = np.exp2(byte - 127.0)
    codes = (blocks / scale).astype(np.float32).astype(dtype).astype(np.float64)
    return np.moveaxis((codes * scale).reshape(v.shape), -1, axis)


WIDE = False


def mx_kscale(k):
    if not WIDE:
        return np.ones(k)
    levels = np.array([10, -10, 5, -5, 0])
    if k % 512:
        return np.exp2(np.random.permutation(np.resize(levels, k // 32))).repeat(32)
    a = np.empty((k // 512, 16))
    for p in range(k // 512):
        a[p, :8] = np.random.permutation(np.resize(levels, 8))
        for g in range(8):
            far = levels[np.abs(levels - a[p, g]) >= 10]
            a[p, g + 8] = far[np.random.randint(len(far))]
    return np.exp2(a.ravel()).repeat(32)


BF16 = ml_dtypes.bfloat16


def bf(x):
    return np.asarray(x, np.float32).astype(BF16)


def f64(x):
    return np.asarray(x).astype(np.float64)


B, T, C, D, P = 8, 2, 512, 512, 128


def draw0():
    s = mx_kscale(C)
    t = mx_kscale(D)
    k = np.random.standard_normal((B, T, C, D)) / np.sqrt(C) * s[:, None]
    w = np.random.standard_normal((B, T, C, D)) * 2.0 / np.sqrt(D) / s[:, None]
    u = np.random.standard_normal((B, T, C, P)) / s[:, None]
    g = np.random.uniform(0.7, 1.0, (B, T, D))
    ga = (1.0 + 0.1 * np.random.standard_normal(D)) * t
    gb = (1.0 + 0.1 * np.random.standard_normal(D)) / t
    return {"k": bf(k), "w": bf(w), "u": bf(u), "g": bf(g), "ga": bf(ga), "gb": bf(gb)}


def chunk_affine_maps(k, w, u, g):
    kt = mxq(k, 2, "e4m3").transpose(0, 1, 3, 2)
    kw = kt @ mxq(w, 2, "e4m3")
    h = kt @ mxq(u, 2, "e4m3")
    m = np.eye(g.shape[-1]) * g[..., :, None] - kw
    return m, h


def core(k, w, u, g, ga, gb):
    m, h = chunk_affine_maps(f64(k), f64(w), f64(u), f64(g))
    m2 = mxq(m[:, 1] * f64(ga)[None, None, :], 2, "e4m3")
    m1 = mxq(m[:, 0] * f64(gb)[None, :, None], 1, "e4m3")
    h1 = mxq(h[:, 0] * f64(gb)[None, :, None], 1, "e4m3")
    mm = m2 @ m1
    hh = (m2 @ h1) + h[:, 1]
    return mm, hh


def e4m3fn_bytes(y):
    return np.clip(np.asarray(y, np.float64), -448.0, 448.0).astype(np.float32).astype(ml_dtypes.float8_e4m3fn).view(np.uint8)


def e4m3fn_values(b):
    return np.asarray(b, np.uint8).view(ml_dtypes.float8_e4m3fn).astype(np.float64)


def setup_inputs():
    d = draw0()
    x0 = np.asarray(d['w']).astype(np.float64)
    s = (np.max(np.abs(x0), axis=(0, 1, 3), keepdims=True) / 448.0).astype(np.float32)
    out = {}
    for k, v in d.items():
        if k == 'w':
            out['w_bytes'] = e4m3fn_bytes(x0 / s.astype(np.float64))
            out['w_scale'] = s
        else:
            out[k] = v
    return out


def reference(k, w_bytes, w_scale, u, g, ga, gb):
    return core(k, e4m3fn_values(w_bytes) * w_scale.astype(np.float64), u, g, ga, gb)

@@ -1,0 +1,387 @@
+from contextlib import ExitStack
+
+import concourse.mybir as mybir
+from concourse.masks import make_identity
+
+B, CH, POS, DIM, COL = 8, 2, 512, 512, 128
+FLOPS = B * 3 * 2 * POS * DIM * (DIM + COL)
+
+F32 = mybir.dt.float32
+BF16 = mybir.dt.bfloat16
+U32 = mybir.dt.uint32
+U8 = mybir.dt.uint8
+FP8 = mybir.dt.float8_e4m3fn
+FP8X4 = mybir.dt.float8_e4m3fn_x4
+MULT = mybir.AluOpType.mult
+ADD = mybir.AluOpType.add
+COPY = mybir.ActivationFunctionType.Copy
+
+P = 128
+T = 4
+ALIGN = 64
+
+
+def tile_gateddeltacontextparallelaffinemerge_t_kernel(
+    tc, k, w_bytes, w_scale, u, g, ga, gb, mm_out, hh_out
+):
+    nc = tc.nc
+    with ExitStack() as ctx:
+        const = ctx.enter_context(tc.tile_pool(name="const", bufs=1))
+        raw = ctx.enter_context(tc.tile_pool(name="raw", bufs=3))
+        work = ctx.enter_context(tc.tile_pool(name="work", bufs=2))
+        quant = ctx.enter_context(tc.tile_pool(name="quant", bufs=2))
+        psum = ctx.enter_context(tc.psum_pool(name="psum", bufs=8))
+        ctx.enter_context(tc.manual_schedule())
+
+        def bank(shape, dtype, name):
+            return psum.tile(shape, dtype, name=name, tag="bank", bufs=8)
+
+        ident = const.tile([P, P], F32, name="ident")
+        ident_bf = const.tile([P, P], BF16, name="ident_bf")
+        rows = const.tile([P, DIM], BF16, name="rows")
+        wsc = const.tile([P, T], F32, name="wsc")
+        coef = const.tile([P, T, 18], F32, name="coef")
+        neg = const.tile([P, T, CH], F32, name="neg")
+        gg = const.tile([P, T, B * CH], F32, name="gg")
+        diag = const.tile([P, B * CH, T, P], F32, name="diag")
+        warm = const.tile([P, 1], F32, name="warm")
+
+        st = [dict() for _ in range(B)]
+
+        def load_w(b, c):
+            t = raw.tile([P, T, DIM], U8, name="w_raw", tag="w_raw", bufs=5, align_bytes=ALIGN)
+            nc.sync.dma_start(out=t[:], in_=w_bytes[b, c].rearrange("(p t) n -> p t n", t=T))
+            st[b]["w_raw", c] = t
+
+        def load_k(b, c):
+            t = raw.tile([P, T, DIM], BF16, name="k_raw", tag="k_raw", bufs=5, align_bytes=ALIGN)
+            nc.sync.dma_start(out=t[:], in_=k[b, c].rearrange("(p t) n -> p t n", t=T))
+            st[b]["k_raw", c] = t
+
+        def load_u(b):
+            t = raw.tile([P, CH, T, COL], BF16, name="u_raw", tag="u_raw", bufs=3, align_bytes=ALIGN)
+            nc.sync.dma_start(out=t[:], in_=u[b].rearrange("c (p t) n -> p c t n", t=T))
+            st[b]["u_raw"] = t
+
+        def widen(b, c, t, eng):
+            if t == 0:
+                st[b]["w_pl", c] = work.tile([P, T, DIM], BF16, name="w_pl", tag="w_pl", bufs=4, align_bytes=ALIGN)
+            src = st[b]["w_raw", c][:, t, :].bitcast(FP8)
+            dst = st[b]["w_pl", c][:, t, :]
+            if eng == "s":
+                nc.scalar.activation(out=dst, in_=src, func=COPY, scale=wsc[:, t : t + 1])
+            else:
+                nc.vector.tensor_scalar(out=dst, in0=src, scalar1=wsc[:, t : t + 1], scalar2=None, op0=MULT)
+
+        def grouped(b, key):
+            st[b]["grp", key] = work.tile([P, DIM * T], BF16, name="grp", tag="grp", bufs=5, align_bytes=ALIGN)
+            return st[b]["grp", key]
+
+        def interleave_perm(b, key, planes):
+            out = grouped(b, key)
+            nc.vector.tensor_copy(
+                out=out[:].rearrange("p (s h l t) -> p h s l t", s=T, l=2, t=T),
+                in_=planes[:].rearrange("p t (h l s) -> p h s l t", l=2, s=T),
+            )
+
+        def interleave_nat(dst, planes):
+            nc.vector.tensor_copy(
+                out=dst.rearrange("p (c i t) -> p c t i", i=4, t=T),
+                in_=planes.rearrange("p t (c i) -> p c t i", i=4),
+            )
+
+        def interleave_u(b, pe):
+            out = work.tile([P, CH * COL * T], BF16, name="grp_u", tag="grp_u", bufs=2, align_bytes=ALIGN)
+            st[b]["grp", "u"] = out
+            if not pe:
+                nc.vector.tensor_copy(
+                    out=out[:].rearrange("p (c n i t) -> p c n t i", c=CH, i=4, t=T),
+                    in_=st[b]["u_raw"][:].rearrange("p c t (n i) -> p c n t i", i=4),
+                )
+                return
+            bk = bank([P, 1024], BF16, "u_bank")
+            for c in range(CH):
+                nc.tensor.matmul(
+                    out=bk[:, c * 512 : (c + 1) * 512].rearrange("p (n t) -> p n t", t=T),
+                    lhsT=ident_bf[:], rhs=st[b]["u_raw"][:, c].rearrange("p t n -> p n t"), start=True, stop=True,
+                )
+            nc.scalar.copy(out=out[:], in_=bk[:])
+
+        def pe_interleave(b, key, planes):
+            view = planes[:].rearrange("p t (m s) -> p s m t", s=T)
+            out = grouped(b, key)
+            st[b]["ilb", key] = []
+            for h in range(2):
+                bk = bank([P, 1024], BF16, "il_bank")
+                for j in range(2):
+                    nc.tensor.matmul(
+                        out=bk[:, j * 512 : (j + 1) * 512].rearrange("p (m t) -> p m t", t=T),
+                        lhsT=ident_bf[:], rhs=view[:, 2 * h + j], start=True, stop=True,
+                    )
+                st[b]["ilb", key].append(bk)
+
+        def pe_interleave_out(b, key, h):
+            nc.scalar.copy(out=st[b]["grp", key][:, h * 1024 : (h + 1) * 1024], in_=st[b]["ilb", key][h][:])
+
+        def quantize(b, key, width, lo=0, hi=None):
+            if lo > 0:
+                q, s = st[b]["q", key]
+                nc.vector.quantize_mx(
+                    out=q[:, lo:width].bitcast(FP8X4), scales=s[:, lo:width], in_=st[b]["grp", key][:, lo * T : width * T]
+                )
+                return
+            hi = hi or width
+            q = quant.tile([P, width], U32, name="q_" + key, tag="q_" + key, bufs=2, align_bytes=ALIGN)
+            s = quant.tile([P, width], U8, name="s_" + key, tag="s_" + key, bufs=2, align_bytes=ALIGN)
+            nc.vector.quantize_mx(out=q[:, 0:hi].bitcast(FP8X4), scales=s[:, 0:hi], in_=st[b]["grp", key][:, 0 : hi * T])
+            st[b]["q", key] = (q, s)
+
+        def mx(out, lhs, lc, rhs, rc, start=True, stop=True):
+            lq, ls = lhs
+            rq, rs = rhs
+            nc.tensor.matmul_mx(
+                out=out, lhsT=lq[:, lc].bitcast(FP8X4), lhsT_scale=ls[:, lc],
+                rhs=rq[:, rc].bitcast(FP8X4), rhs_scale=rs[:, rc], start=start, stop=stop,
+            )
+
+        def blk(i):
+            return slice(i * P, (i + 1) * P)
+
+        ALLC = slice(0, DIM)
+
+        def map_x(b, c):
+            lhs, rhs = (st[b]["q", "k0"], st[b]["q", "w0"]) if c == 0 else (st[b]["q", "w1"], st[b]["q", "k1"])
+            bk = bank([P, T, P], F32, "x_bank")
+            for t in range(T):
+                mx(bk[:, t, :], lhs, blk(t), rhs, blk(t))
+            st[b]["x", c] = bk
+
+        def map_t(b, c, t):
+            lhs, rhs = (st[b]["q", "k0"], st[b]["q", "w0"]) if c == 0 else (st[b]["q", "w1"], st[b]["q", "k1"])
+            bk = bank([P, DIM], F32, "m_bank")
+            mx(bk[:], lhs, blk(t), rhs, ALLC)
+            if t == 0:
+                st[b]["pl", c] = work.tile([P, T, DIM], BF16, name="m_pl", tag="m_pl", bufs=3, align_bytes=ALIGN)
+            st[b]["mb", c, t] = bk
+
+        def map_h(b):
+            bk = bank([P, T, COL], F32, "h_bank")
+            for t in range(T):
+                mx(bk[:, t, :], st[b]["q", "k0"], blk(t), st[b]["q", "u"], blk(0))
+            st[b]["hb"] = bk
+
+        def plane_out(b, c, t, eng="s"):
+            for lo, hi in ((0, t * P), ((t + 1) * P, DIM)):
+                if hi > lo:
+                    dst = st[b]["pl", c][:, t, lo:hi]
+                    src = st[b]["mb", c, t][:, lo:hi]
+                    if eng == "s":
+                        nc.scalar.activation(out=dst, in_=src, func=COPY, scale=neg[:, t, c : c + 1])
+                    else:
+                        nc.vector.tensor_scalar(out=dst, in0=src, scalar1=neg[:, t, c : c + 1], scalar2=None, op0=MULT)
+
+        def diag_out(b, c):
+            for t in range(T):
+                nc.vector.scalar_tensor_tensor(
+                    out=st[b]["pl", c][:, t, blk(t)], in0=st[b]["x", c][:, t, :], scalar=neg[:, t, c : c + 1],
+                    in1=diag[:, 2 * b + c, t, :], op0=MULT, op1=ADD,
+                )
+
+        def h_out(b):
+            out = work.tile([P, COL * T], BF16, name="grp_h", tag="grp_h", bufs=2, align_bytes=ALIGN)
+            nc.vector.tensor_tensor(
+                out=out[:].rearrange("p (n t) -> p n t", t=T),
+                in0=st[b]["hb"][:].rearrange("p t n -> p n t"),
+                in1=coef[:, :, 16].unsqueeze(1).to_broadcast([P, COL, T]),
+                op=MULT,
+            )
+            st[b]["grp", "h"] = out
+
+        def interleave_m(b, c, lo=0, hi=DIM):
+            if lo == 0:
+                st[b]["grp", "m%d" % c] = work.tile([P, DIM * T], BF16, name="grp_m", tag="grp_m", bufs=3, align_bytes=ALIGN)
+            interleave_nat(st[b]["grp", "m%d" % c][:, lo * T : hi * T], st[b]["pl", c][:, :, lo:hi])
+
+        def build_diag(b, c, eng="v"):
+            for t in range(T):
+                dst = diag[:, 2 * b + c, t, :]
+                col = gg[:, t, 2 * b + c : 2 * b + c + 1]
+                if eng == "v":
+                    nc.vector.tensor_scalar(out=dst, in0=ident[:], scalar1=col, scalar2=None, op0=MULT)
+                else:
+                    nc.scalar.activation(out=dst, in_=ident[:], func=COPY, scale=col)
+
+        def merge(b, s):
+            bk = bank([P, DIM], F32, "o_bank")
+            mx(bk[:], st[b]["q", "m1"], blk(s), st[b]["q", "m0"], ALLC)
+            st[b]["ob", s] = bk
+
+        def merge_h(b, lo=0, hi=T):
+            if lo == 0:
+                st[b]["ohb"] = bank([P, T, COL], F32, "oh_bank")
+            bk = st[b]["ohb"]
+            for s in range(lo, hi):
+                mx(bk[:, s, :], st[b]["q", "k1"], blk(s), st[b]["q", "u"], blk(1), True, False)
+                mx(bk[:, s, :], st[b]["q", "m1"], blk(s), st[b]["q", "h"], blk(0), False, True)
+
+        def merge_out(b, s, eng="s"):
+            if s == 0:
+                st[b]["o"] = work.tile([P, T, DIM], F32, name="o_sb", tag="o_sb", bufs=2, align_bytes=ALIGN)
+            dst = st[b]["o"][:, s, :].rearrange("p (m j) -> p m j", j=T)
+            src = st[b]["ob", s][:].rearrange("p (j m) -> p m j", j=T)
+            if eng == "s":
+                nc.scalar.copy(out=dst, in_=src)
+            else:
+                nc.vector.tensor_copy(out=dst, in_=src)
+
+        def merge_h_out(b, eng="s"):
+            o = work.tile([P, T, COL], F32, name="oh_sb", tag="oh_sb", bufs=2, align_bytes=ALIGN)
+            if eng == "s":
+                nc.scalar.copy(out=o[:], in_=st[b]["ohb"][:])
+            else:
+                nc.vector.tensor_copy(out=o[:], in_=st[b]["ohb"][:])
+            st[b]["oh"] = o
+
+        def store(b, lo, hi):
+            nc.sync.dma_start(out=mm_out[b].rearrange("(m s) f -> m s f", s=T)[:, lo:hi, :], in_=st[b]["o"][:, lo:hi, :])
+
+        def store_h(b):
+            nc.sync.dma_start(out=hh_out[b].rearrange("(m s) f -> m s f", s=T), in_=st[b]["oh"][:])
+
+        nc.vector.memset(rows[:], 0.0)
+        nc.vector.memset(warm[:], 0.0)
+        make_identity(nc, ident_bf[:])
+        make_identity(nc, ident[:])
+        nc.scalar.dma_start(out=wsc[:], in_=w_scale.rearrange("a b (p t) o -> p (a b t o)", t=T))
+        nc.scalar.dma_start(out=rows[0:16, :], in_=g.rearrange("b c d -> (b c) d"))
+        nc.scalar.dma_start(out=rows[16:17, :], in_=gb.unsqueeze(0))
+        nc.scalar.dma_start(out=rows[17:18, :], in_=ga.unsqueeze(0))
+        nc.scalar.activation(out=warm[:], in_=warm[:], func=COPY)
+        load_w(0, 0)
+        load_k(0, 0)
+        load_u(0)
+        load_w(0, 1)
+        load_k(0, 1)
+        load_w(1, 0)
+        load_k(1, 0)
+        load_u(1)
+        load_w(1, 1)
+        load_k(1, 1)
+
+
+        for t in range(T):
+            widen(0, 0, t, "s" if t == 0 else "v")
+        pe_interleave(0, "k0", st[0]["k_raw", 0])
+        interleave_perm(0, "w0", st[0]["w_pl", 0])
+        tb = bank([P, T, P], BF16, "t_bank")
+        for t in range(T):
+            nc.tensor.transpose(tb[:, t, :], rows[:].rearrange("r (m t) -> r t m", t=T)[:, t, :], ident_bf[:])
+        pe_interleave_out(0, "k0", 0)
+        pe_interleave_out(0, "k0", 1)
+        interleave_u(0, False)
+        quantize(0, "w0", DIM)
+        quantize(0, "k0", DIM)
+        nc.vector.tensor_copy(out=coef[:], in_=tb[:, :, 0:18])
+        nc.vector.tensor_scalar(out=neg[:], in0=coef[:, :, 16:18], scalar1=-1.0, scalar2=None, op0=MULT)
+        quantize(0, "u", CH * COL)
+        nc.vector.tensor_tensor(
+            out=gg[:].rearrange("p t (b c) -> p t b c", c=CH),
+            in0=coef[:, :, 0:16].rearrange("p t (b c) -> p t b c", c=CH),
+            in1=coef[:, :, 16:18].unsqueeze(2).to_broadcast([P, T, B, CH]),
+            op=MULT,
+        )
+        for t in range(T):
+            widen(0, 1, t, "s")
+        build_diag(0, 0, "s")
+        interleave_perm(0, "k1", st[0]["k_raw", 1])
+        interleave_perm(0, "w1", st[0]["w_pl", 1])
+        quantize(0, "k1", DIM)
+        quantize(0, "w1", DIM)
+
+        for b in range(B):
+            n = b + 1
+            nx = n < B
+            if b + 2 < B:
+                load_w(b + 2, 0)
+                load_k(b + 2, 0)
+                load_u(b + 2)
+                load_w(b + 2, 1)
+                load_k(b + 2, 1)
+            map_x(b, 0)
+            for t in range(T):
+                map_t(b, 0, t)
+            map_h(b)
+            if nx:
+                interleave_perm(n, "k1", st[n]["k_raw", 1])
+            for t in range(T):
+                plane_out(b, 0, t)
+            if b == 0:
+                build_diag(0, 1, "s")
+            diag_out(b, 0)
+            h_out(b)
+            map_x(b, 1)
+            for t in range(T):
+                map_t(b, 1, t)
+            if nx:
+                quantize(n, "k1", DIM)
+            interleave_m(b, 0)
+            for t in range(T):
+                if not nx and t == 0:
+                    merge_out(b - 1, 0)
+                    merge_out(b - 1, 1)
+                    store(b - 1, 0, 2)
+                plane_out(b, 1, t)
+            if not nx:
+                merge_out(b - 1, 2)
+                merge_out(b - 1, 3)
+                store(b - 1, 2, 4)
+                merge_h_out(b - 1)
+                store_h(b - 1)
+            diag_out(b, 1)
+            quantize(b, "m0", DIM)
+            if nx:
+                for t in range(T):
+                    widen(n, 0, t, "s")
+                interleave_m(b, 1)
+                quantize(b, "h", COL)
+                interleave_perm(n, "w0", st[n]["w_pl", 0])
+                quantize(b, "m1", DIM)
+                interleave_u(n, n < 8)
+                pe_interleave(n, "k0", st[n]["k_raw", 0])
+                pe_interleave_out(n, "k0", 0)
+                pe_interleave_out(n, "k0", 1)
+                quantize(n, "w0", DIM)
+                for t in range(T):
+                    widen(n, 1, t, "v" if t == 3 and n % 3 else "s")
+                quantize(n, "u", CH * COL)
+                build_diag(n, 0)
+                quantize(n, "k0", DIM)
+                interleave_perm(n, "w1", st[n]["w_pl", 1])
+                build_diag(n, 1)
+                quantize(n, "w1", DIM)
+            else:
+                interleave_m(b, 1, 0, 256)
+                quantize(b, "h", COL)
+                quantize(b, "m1", DIM, 0, 256)
+                interleave_m(b, 1, 256, DIM)
+                quantize(b, "m1", DIM, 256)
+            if nx:
+                for s in range(T):
+                    merge(b, s)
+                merge_h(b)
+                if b + 2 < B:
+                    for s in range(T):
+                        merge_out(b, s)
+                        if s % 2 == 1:
+                            store(b, s - 1, s + 1)
+                    merge_h_out(b)
+                    store_h(b)
+            else:
+                for s in range(T):
+                    merge(b, s)
+                    if s % 2 == 1:
+                        merge_h(b, s - 1, s + 1)
+                    merge_out(b, s, "v" if s % 2 else "s")
+                    store(b, s, s + 1)
+                merge_h_out(b)
+                store_h(b)

@@ -80,8 +80,8 @@ def tile_gateddeltacontextparallelaffinemerge_t_kernel(
         def interleave_perm(b, key, planes):
             out = grouped(b, key)
             nc.vector.tensor_copy(
-                out=out[:].rearrange("p (s h l t) -> p h s l t", s=T, l=2, t=T),
-                in_=planes[:].rearrange("p t (h l s) -> p h s l t", l=2, s=T),
+                out=out[:].rearrange("p (s m t) -> p m t s", s=T, t=T),
+                in_=planes[:].rearrange("p t (m s) -> p m t s", s=T),
             )
 
         def interleave_nat(dst, planes):
@@ -311,13 +311,13 @@ def tile_gateddeltacontextparallelaffinemerge_t_kernel(
             for t in range(T):
                 map_t(b, 0, t)
             map_h(b)
-            if nx:
-                interleave_perm(n, "k1", st[n]["k_raw", 1])
             for t in range(T):
                 plane_out(b, 0, t)
             if b == 0:
                 build_diag(0, 1, "s")
             diag_out(b, 0)
+            if nx:
+                interleave_perm(n, "k1", st[n]["k_raw", 1])
             h_out(b)
             map_x(b, 1)
             for t in range(T):
@@ -352,7 +352,7 @@ def tile_gateddeltacontextparallelaffinemerge_t_kernel(
                 pe_interleave_out(n, "k0", 1)
                 quantize(n, "w0", DIM)
                 for t in range(T):
-                    widen(n, 1, t, "v" if t == 3 and n % 3 else "s")
+                    widen(n, 1, t, "s")
                 quantize(n, "u", CH * COL)
                 build_diag(n, 0)
                 quantize(n, "k0", DIM)

@@ -19,6 +19,9 @@ COPY = mybir.ActivationFunctionType.Copy
 P = 128
 T = 4
 ALIGN = 64
+MATS = CH * T
+SEED = 8
+PITCH = P + SEED
 
 
 def tile_gateddeltacontextparallelaffinemerge_t_kernel(
@@ -42,8 +45,8 @@ def tile_gateddeltacontextparallelaffinemerge_t_kernel(
         wsc = const.tile([P, T], F32, name="wsc")
         coef = const.tile([P, T, 18], F32, name="coef")
         neg = const.tile([P, T, CH], F32, name="neg")
-        gg = const.tile([P, T, B * CH], F32, name="gg")
-        diag = const.tile([P, B * CH, T, P], F32, name="diag")
+        seed = const.tile([P, B * CH * T, SEED], F32, name="seed")
+        zeros = const.tile([P, MATS * PITCH], F32, name="zeros")
         warm = const.tile([P, 1], F32, name="warm")
 
         st = [dict() for _ in range(B)]
@@ -84,8 +87,8 @@ def tile_gateddeltacontextparallelaffinemerge_t_kernel(
                 in_=planes[:].rearrange("p t (m s) -> p m t s", s=T),
             )
 
-        def interleave_nat(dst, planes):
-            nc.vector.tensor_copy(
+        def interleave_nat(dst, planes, eng):
+            (nc.vector.tensor_copy if eng == "v" else nc.scalar.copy)(
                 out=dst.rearrange("p (c i t) -> p c t i", i=4, t=T),
                 in_=planes.rearrange("p t (c i) -> p c t i", i=4),
             )
@@ -184,7 +187,7 @@ def tile_gateddeltacontextparallelaffinemerge_t_kernel(
             for t in range(T):
                 nc.vector.scalar_tensor_tensor(
                     out=st[b]["pl", c][:, t, blk(t)], in0=st[b]["x", c][:, t, :], scalar=neg[:, t, c : c + 1],
-                    in1=diag[:, 2 * b + c, t, :], op0=MULT, op1=ADD,
+                    in1=st[b]["diag"][:, c * T + t, :], op0=MULT, op1=ADD,
                 )
 
         def h_out(b):
@@ -197,19 +200,35 @@ def tile_gateddeltacontextparallelaffinemerge_t_kernel(
             )
             st[b]["grp", "h"] = out
 
-        def interleave_m(b, c, lo=0, hi=DIM):
+        def interleave_m(b, c, lo=0, hi=DIM, eng="v"):
             if lo == 0:
                 st[b]["grp", "m%d" % c] = work.tile([P, DIM * T], BF16, name="grp_m", tag="grp_m", bufs=3, align_bytes=ALIGN)
-            interleave_nat(st[b]["grp", "m%d" % c][:, lo * T : hi * T], st[b]["pl", c][:, :, lo:hi])
+            interleave_nat(st[b]["grp", "m%d" % c][:, lo * T : hi * T], st[b]["pl", c][:, :, lo:hi], eng)
 
-        def build_diag(b, c, eng="v"):
+        park = mm_out[B - 1].rearrange("d f -> (d f)")[0 : MATS * P * PITCH]
+
+        def diag_tile(b):
+            st[b]["diag"] = work.tile([P, MATS, P], F32, name="diag", tag="diag", bufs=3, align_bytes=ALIGN)
+
+        def build_diag(b, c):
             for t in range(T):
-                dst = diag[:, 2 * b + c, t, :]
-                col = gg[:, t, 2 * b + c : 2 * b + c + 1]
-                if eng == "v":
-                    nc.vector.tensor_scalar(out=dst, in0=ident[:], scalar1=col, scalar2=None, op0=MULT)
-                else:
-                    nc.scalar.activation(out=dst, in_=ident[:], func=COPY, scale=col)
+                i = c * T + t
+                nc.scalar.activation(
+                    out=st[b]["diag"][:, i, :], in_=ident[:], func=COPY, scale=seed[:, b * MATS + i, 0:1]
+                )
+
+        def park_seed(b):
+            nc.sync.dma_start(
+                out=park.rearrange("(i p w) -> p i w", p=P, w=PITCH)[:, :, 0:SEED],
+                in_=seed[:, b * MATS : (b + 1) * MATS, :],
+            )
+
+        def load_diag(b):
+            diag_tile(b)
+            nc.sync.dma_start(
+                out=st[b]["diag"][:],
+                in_=park.rearrange("(i x) -> i x", i=MATS)[:, 0 : P * (PITCH - 1)].rearrange("i (p w) -> p i w", p=P)[:, :, 0:P],
+            )
 
         def merge(b, s):
             bk = bank([P, DIM], F32, "o_bank")
@@ -252,6 +271,8 @@ def tile_gateddeltacontextparallelaffinemerge_t_kernel(
         nc.vector.memset(warm[:], 0.0)
         make_identity(nc, ident_bf[:])
         make_identity(nc, ident[:])
+        nc.gpsimd.memset(seed[:], 0.0)
+        nc.gpsimd.memset(zeros[:], 0.0)
         nc.scalar.dma_start(out=wsc[:], in_=w_scale.rearrange("a b (p t) o -> p (a b t o)", t=T))
         nc.scalar.dma_start(out=rows[0:16, :], in_=g.rearrange("b c d -> (b c) d"))
         nc.scalar.dma_start(out=rows[16:17, :], in_=gb.unsqueeze(0))
@@ -267,6 +288,7 @@ def tile_gateddeltacontextparallelaffinemerge_t_kernel(
         load_u(1)
         load_w(1, 1)
         load_k(1, 1)
+        nc.sync.dma_start(out=park.rearrange("(p x) -> p x", p=P), in_=zeros[:])
 
 
         for t in range(T):
@@ -285,14 +307,15 @@ def tile_gateddeltacontextparallelaffinemerge_t_kernel(
         nc.vector.tensor_scalar(out=neg[:], in0=coef[:, :, 16:18], scalar1=-1.0, scalar2=None, op0=MULT)
         quantize(0, "u", CH * COL)
         nc.vector.tensor_tensor(
-            out=gg[:].rearrange("p t (b c) -> p t b c", c=CH),
+            out=seed[:, :, 0].rearrange("p (b c t) -> p t b c", c=CH, t=T),
             in0=coef[:, :, 0:16].rearrange("p t (b c) -> p t b c", c=CH),
             in1=coef[:, :, 16:18].unsqueeze(2).to_broadcast([P, T, B, CH]),
             op=MULT,
         )
         for t in range(T):
             widen(0, 1, t, "s")
-        build_diag(0, 0, "s")
+        diag_tile(0)
+        build_diag(0, 0)
         interleave_perm(0, "k1", st[0]["k_raw", 1])
         interleave_perm(0, "w1", st[0]["w_pl", 1])
         quantize(0, "k1", DIM)
@@ -301,20 +324,30 @@ def tile_gateddeltacontextparallelaffinemerge_t_kernel(
         for b in range(B):
             n = b + 1
             nx = n < B
+            if b == 0:
+                park_seed(1)
+                load_diag(1)
             if b + 2 < B:
+                park_seed(b + 2)
                 load_w(b + 2, 0)
                 load_k(b + 2, 0)
                 load_u(b + 2)
                 load_w(b + 2, 1)
                 load_k(b + 2, 1)
+                load_diag(b + 2)
             map_x(b, 0)
             for t in range(T):
                 map_t(b, 0, t)
             map_h(b)
+            if not nx:
+                for s in range(T):
+                    merge_out(b - 1, s)
+                    if s % 2 == 1:
+                        store(b - 1, s - 1, s + 1)
             for t in range(T):
                 plane_out(b, 0, t)
             if b == 0:
-                build_diag(0, 1, "s")
+                build_diag(0, 1)
             diag_out(b, 0)
             if nx:
                 interleave_perm(n, "k1", st[n]["k_raw", 1])
@@ -325,18 +358,11 @@ def tile_gateddeltacontextparallelaffinemerge_t_kernel(
             if nx:
                 quantize(n, "k1", DIM)
             interleave_m(b, 0)
-            for t in range(T):
-                if not nx and t == 0:
-                    merge_out(b - 1, 0)
-                    merge_out(b - 1, 1)
-                    store(b - 1, 0, 2)
-                plane_out(b, 1, t)
             if not nx:
-                merge_out(b - 1, 2)
-                merge_out(b - 1, 3)
-                store(b - 1, 2, 4)
                 merge_h_out(b - 1)
                 store_h(b - 1)
+            for t in range(T):
+                plane_out(b, 1, t)
             diag_out(b, 1)
             quantize(b, "m0", DIM)
             if nx:
@@ -352,18 +378,16 @@ def tile_gateddeltacontextparallelaffinemerge_t_kernel(
                 pe_interleave_out(n, "k0", 1)
                 quantize(n, "w0", DIM)
                 for t in range(T):
-                    widen(n, 1, t, "s")
+                    widen(n, 1, t, "v" if t == 3 else "s")
                 quantize(n, "u", CH * COL)
-                build_diag(n, 0)
-                quantize(n, "k0", DIM)
                 interleave_perm(n, "w1", st[n]["w_pl", 1])
-                build_diag(n, 1)
+                quantize(n, "k0", DIM)
                 quantize(n, "w1", DIM)
             else:
                 interleave_m(b, 1, 0, 256)
                 quantize(b, "h", COL)
                 quantize(b, "m1", DIM, 0, 256)
-                interleave_m(b, 1, 256, DIM)
+                interleave_m(b, 1, 256, DIM, "s")
                 quantize(b, "m1", DIM, 256)
             if nx:
                 for s in range(T):

@@ -57,12 +57,12 @@ def tile_gateddeltacontextparallelaffinemerge_t_kernel(
             st[b]["w_raw", c] = t
 
         def load_k(b, c):
-            t = raw.tile([P, T, DIM], BF16, name="k_raw", tag="k_raw", bufs=5, align_bytes=ALIGN)
+            t = raw.tile([P, T, DIM], BF16, name="k_raw", tag="k_raw", bufs=6, align_bytes=ALIGN)
             nc.sync.dma_start(out=t[:], in_=k[b, c].rearrange("(p t) n -> p t n", t=T))
             st[b]["k_raw", c] = t
 
         def load_u(b):
-            t = raw.tile([P, CH, T, COL], BF16, name="u_raw", tag="u_raw", bufs=3, align_bytes=ALIGN)
+            t = raw.tile([P, CH, T, COL], BF16, name="u_raw", tag="u_raw", bufs=4, align_bytes=ALIGN)
             nc.sync.dma_start(out=t[:], in_=u[b].rearrange("c (p t) n -> p c t n", t=T))
             st[b]["u_raw"] = t
 
@@ -77,12 +77,13 @@ def tile_gateddeltacontextparallelaffinemerge_t_kernel(
                 nc.vector.tensor_scalar(out=dst, in0=src, scalar1=wsc[:, t : t + 1], scalar2=None, op0=MULT)
 
         def grouped(b, key):
-            st[b]["grp", key] = work.tile([P, DIM * T], BF16, name="grp", tag="grp", bufs=5, align_bytes=ALIGN)
+            tag = "grp_k0" if key == "k0" else "grp"
+            st[b]["grp", key] = work.tile([P, DIM * T], BF16, name=tag, tag=tag, bufs=3, align_bytes=ALIGN)
             return st[b]["grp", key]
 
-        def interleave_perm(b, key, planes):
+        def interleave_perm(b, key, planes, eng="v"):
             out = grouped(b, key)
-            nc.vector.tensor_copy(
+            (nc.vector.tensor_copy if eng == "v" else nc.scalar.copy)(
                 out=out[:].rearrange("p (s m t) -> p m t s", s=T, t=T),
                 in_=planes[:].rearrange("p t (m s) -> p m t s", s=T),
             )
@@ -94,7 +95,7 @@ def tile_gateddeltacontextparallelaffinemerge_t_kernel(
             )
 
         def interleave_u(b, pe):
-            out = work.tile([P, CH * COL * T], BF16, name="grp_u", tag="grp_u", bufs=2, align_bytes=ALIGN)
+            out = work.tile([P, CH * COL * T], BF16, name="grp_u", tag="grp_u", bufs=3, align_bytes=ALIGN)
             st[b]["grp", "u"] = out
             if not pe:
                 nc.vector.tensor_copy(
@@ -205,7 +206,7 @@ def tile_gateddeltacontextparallelaffinemerge_t_kernel(
                 st[b]["grp", "m%d" % c] = work.tile([P, DIM * T], BF16, name="grp_m", tag="grp_m", bufs=3, align_bytes=ALIGN)
             interleave_nat(st[b]["grp", "m%d" % c][:, lo * T : hi * T], st[b]["pl", c][:, :, lo:hi], eng)
 
-        park = mm_out[B - 1].rearrange("d f -> (d f)")[0 : MATS * P * PITCH]
+        parks = [mm_out[B - 1 - i].rearrange("d f -> (d f)")[0 : MATS * P * PITCH] for i in range(2)]
 
         def diag_tile(b):
             st[b]["diag"] = work.tile([P, MATS, P], F32, name="diag", tag="diag", bufs=3, align_bytes=ALIGN)
@@ -219,7 +220,7 @@ def tile_gateddeltacontextparallelaffinemerge_t_kernel(
 
         def park_seed(b):
             nc.sync.dma_start(
-                out=park.rearrange("(i p w) -> p i w", p=P, w=PITCH)[:, :, 0:SEED],
+                out=parks[b % 2].rearrange("(i p w) -> p i w", p=P, w=PITCH)[:, :, 0:SEED],
                 in_=seed[:, b * MATS : (b + 1) * MATS, :],
             )
 
@@ -227,7 +228,7 @@ def tile_gateddeltacontextparallelaffinemerge_t_kernel(
             diag_tile(b)
             nc.sync.dma_start(
                 out=st[b]["diag"][:],
-                in_=park.rearrange("(i x) -> i x", i=MATS)[:, 0 : P * (PITCH - 1)].rearrange("i (p w) -> p i w", p=P)[:, :, 0:P],
+                in_=parks[b % 2].rearrange("(i x) -> i x", i=MATS)[:, 0 : P * (PITCH - 1)].rearrange("i (p w) -> p i w", p=P)[:, :, 0:P],
             )
 
         def merge(b, s):
@@ -288,8 +289,11 @@ def tile_gateddeltacontextparallelaffinemerge_t_kernel(
         load_u(1)
         load_w(1, 1)
         load_k(1, 1)
-        nc.sync.dma_start(out=park.rearrange("(p x) -> p x", p=P), in_=zeros[:])
-
+        load_w(2, 0)
+        load_k(2, 0)
+        load_u(2)
+        for park in parks:
+            nc.sync.dma_start(out=park.rearrange("(p x) -> p x", p=P), in_=zeros[:])
 
         for t in range(T):
             widen(0, 0, t, "s" if t == 0 else "v")
@@ -302,6 +306,7 @@ def tile_gateddeltacontextparallelaffinemerge_t_kernel(
         pe_interleave_out(0, "k0", 1)
         interleave_u(0, False)
         quantize(0, "w0", DIM)
+        interleave_perm(0, "k1", st[0]["k_raw", 1])
         quantize(0, "k0", DIM)
         nc.vector.tensor_copy(out=coef[:], in_=tb[:, :, 0:18])
         nc.vector.tensor_scalar(out=neg[:], in0=coef[:, :, 16:18], scalar1=-1.0, scalar2=None, op0=MULT)
@@ -316,91 +321,128 @@ def tile_gateddeltacontextparallelaffinemerge_t_kernel(
             widen(0, 1, t, "s")
         diag_tile(0)
         build_diag(0, 0)
-        interleave_perm(0, "k1", st[0]["k_raw", 1])
+        V_PLANES = [(b, 1, 3) for b in range(2, B)] + [(1, 0, 2), (1, 0, 3), (2, 0, 1), (2, 0, 2)]
+
+        def widen_all(b, c):
+            for t in range(T):
+                widen(b, c, t, "v" if (b, c, t) in V_PLANES else "s")
+
+        def lead_inputs(b):
+            interleave_u(b, True)
+            pe_interleave(b, "k0", st[b]["k_raw", 0])
+            pe_interleave_out(b, "k0", 0)
+            pe_interleave_out(b, "k0", 1)
+
+        map_x(0, 0)
+        for t in range(T):
+            map_t(0, 0, t)
+        map_h(0)
+        for t in range(T):
+            plane_out(0, 0, t)
         interleave_perm(0, "w1", st[0]["w_pl", 1])
+        build_diag(0, 1)
+        diag_out(0, 0)
         quantize(0, "k1", DIM)
+        h_out(0)
         quantize(0, "w1", DIM)
+        widen_all(1, 0)
+        lead_inputs(1)
 
         for b in range(B):
             n = b + 1
             nx = n < B
-            if b == 0:
+            lead = b + 2 < B
+            first = b == 0
+            if first:
                 park_seed(1)
-                load_diag(1)
-            if b + 2 < B:
-                park_seed(b + 2)
-                load_w(b + 2, 0)
-                load_k(b + 2, 0)
-                load_u(b + 2)
+                park_seed(2)
+            if lead:
                 load_w(b + 2, 1)
                 load_k(b + 2, 1)
+            if b + 3 < B:
+                load_w(b + 3, 0)
+                load_k(b + 3, 0)
+                load_u(b + 3)
+            if first:
+                load_diag(1)
+            if lead:
                 load_diag(b + 2)
-            map_x(b, 0)
-            for t in range(T):
-                map_t(b, 0, t)
-            map_h(b)
-            if not nx:
-                for s in range(T):
-                    merge_out(b - 1, s)
-                    if s % 2 == 1:
-                        store(b - 1, s - 1, s + 1)
-            for t in range(T):
-                plane_out(b, 0, t)
-            if b == 0:
-                build_diag(0, 1)
-            diag_out(b, 0)
-            if nx:
-                interleave_perm(n, "k1", st[n]["k_raw", 1])
-            h_out(b)
+            if b + 3 < B:
+                park_seed(b + 3)
+            early = 2 if not nx else 0 if first else T
+            for s in range(early):
+                merge(b - 1, s)
+            if nx and not first:
+                merge_h(b - 1)
             map_x(b, 1)
             for t in range(T):
                 map_t(b, 1, t)
-            if nx:
-                quantize(n, "k1", DIM)
-            interleave_m(b, 0)
+            for s in range(early):
+                merge_out(b - 1, s)
+                if s % 2 == 1:
+                    store(b - 1, s - 1, s + 1)
             if not nx:
+                for t in range(T):
+                    plane_out(b, 1, t)
+                for s in range(early, T):
+                    merge(b - 1, s)
+                merge_h(b - 1)
+                for s in range(early, T):
+                    merge_out(b - 1, s)
+                store(b - 1, early, T)
+            if not first:
                 merge_h_out(b - 1)
                 store_h(b - 1)
-            for t in range(T):
-                plane_out(b, 1, t)
-            diag_out(b, 1)
-            quantize(b, "m0", DIM)
             if nx:
                 for t in range(T):
-                    widen(n, 0, t, "s")
-                interleave_m(b, 1)
-                quantize(b, "h", COL)
-                interleave_perm(n, "w0", st[n]["w_pl", 0])
-                quantize(b, "m1", DIM)
-                interleave_u(n, n < 8)
-                pe_interleave(n, "k0", st[n]["k_raw", 0])
-                pe_interleave_out(n, "k0", 0)
-                pe_interleave_out(n, "k0", 1)
-                quantize(n, "w0", DIM)
-                for t in range(T):
-                    widen(n, 1, t, "v" if t == 3 else "s")
-                quantize(n, "u", CH * COL)
-                interleave_perm(n, "w1", st[n]["w_pl", 1])
+                    plane_out(b, 1, t)
+                if first:
+                    interleave_perm(n, "k1", st[n]["k_raw", 1])
+                else:
+                    interleave_perm(n, "w0", st[n]["w_pl", 0])
+                diag_out(b, 1)
+                interleave_m(b, 0)
+                quantize(n, "k1" if first else "w0", DIM)
+                quantize(b, "m0", DIM)
+                widen_all(n, 1)
+                if first:
+                    interleave_perm(n, "w0", st[n]["w_pl", 0])
+                else:
+                    interleave_perm(n, "k1", st[n]["k_raw", 1], "s" if n == B - 1 else "v")
                 quantize(n, "k0", DIM)
+                if first:
+                    quantize(n, "w0", DIM)
+                quantize(n, "u", CH * COL)
+                quantize(b, "h", COL)
+                if lead:
+                    lead_inputs(b + 2)
+                interleave_m(b, 1)
+                if lead and not first:
+                    quantize(n, "k1", DIM)
+                interleave_perm(n, "w1", st[n]["w_pl", 1])
+                if lead:
+                    widen_all(b + 2, 0)
+                quantize(b, "m1", DIM)
+                if not lead:
+                    quantize(n, "k1", DIM)
+                map_x(n, 0)
+                for t in range(T):
+                    map_t(n, 0, t)
+                map_h(n)
+                for t in range(T):
+                    plane_out(n, 0, t)
                 quantize(n, "w1", DIM)
+                diag_out(n, 0)
+                h_out(n)
             else:
+                interleave_m(b, 0)
+                diag_out(b, 1)
+                quantize(b, "m0", DIM)
                 interleave_m(b, 1, 0, 256)
                 quantize(b, "h", COL)
                 quantize(b, "m1", DIM, 0, 256)
-                interleave_m(b, 1, 256, DIM, "s")
+                interleave_m(b, 1, 256, DIM)
                 quantize(b, "m1", DIM, 256)
-            if nx:
-                for s in range(T):
-                    merge(b, s)
-                merge_h(b)
-                if b + 2 < B:
-                    for s in range(T):
-                        merge_out(b, s)
-                        if s % 2 == 1:
-                            store(b, s - 1, s + 1)
-                    merge_h_out(b)
-                    store_h(b)
-            else:
                 for s in range(T):
                     merge(b, s)
                     if s % 2 == 1:

from contextlib import ExitStack

import concourse.mybir as mybir
from concourse.masks import make_identity

B, CH, POS, DIM, COL = 8, 2, 512, 512, 128
FLOPS = B * 3 * 2 * POS * DIM * (DIM + COL)

F32 = mybir.dt.float32
BF16 = mybir.dt.bfloat16
U32 = mybir.dt.uint32
U8 = mybir.dt.uint8
FP8 = mybir.dt.float8_e4m3fn
FP8X4 = mybir.dt.float8_e4m3fn_x4
MULT = mybir.AluOpType.mult
ADD = mybir.AluOpType.add
COPY = mybir.ActivationFunctionType.Copy

P = 128
T = 4
ALIGN = 64
MATS = CH * T
SEED = 8
PITCH = P + SEED


def tile_gateddeltacontextparallelaffinemerge_t_kernel(
    tc, k, w_bytes, w_scale, u, g, ga, gb, mm_out, hh_out
):
    nc = tc.nc
    with ExitStack() as ctx:
        const = ctx.enter_context(tc.tile_pool(name="const", bufs=1))
        raw = ctx.enter_context(tc.tile_pool(name="raw", bufs=3))
        work = ctx.enter_context(tc.tile_pool(name="work", bufs=2))
        quant = ctx.enter_context(tc.tile_pool(name="quant", bufs=2))
        psum = ctx.enter_context(tc.psum_pool(name="psum", bufs=8))
        ctx.enter_context(tc.manual_schedule())

        def bank(shape, dtype, name):
            return psum.tile(shape, dtype, name=name, tag="bank", bufs=8)

        ident = const.tile([P, P], F32, name="ident")
        ident_bf = const.tile([P, P], BF16, name="ident_bf")
        rows = const.tile([P, DIM], BF16, name="rows")
        wsc = const.tile([P, T], F32, name="wsc")
        coef = const.tile([P, T, 18], F32, name="coef")
        neg = const.tile([P, T, CH], F32, name="neg")
        seed = const.tile([P, B * CH * T, SEED], F32, name="seed")
        zeros = const.tile([P, MATS * PITCH], F32, name="zeros")
        warm = const.tile([P, 1], F32, name="warm")

        st = [dict() for _ in range(B)]

        def load_w(b, c):
            t = raw.tile([P, T, DIM], U8, name="w_raw", tag="w_raw", bufs=5, align_bytes=ALIGN)
            nc.sync.dma_start(out=t[:], in_=w_bytes[b, c].rearrange("(p t) n -> p t n", t=T))
            st[b]["w_raw", c] = t

        def load_k(b, c):
            t = raw.tile([P, T, DIM], BF16, name="k_raw", tag="k_raw", bufs=6, align_bytes=ALIGN)
            nc.sync.dma_start(out=t[:], in_=k[b, c].rearrange("(p t) n -> p t n", t=T))
            st[b]["k_raw", c] = t

        def load_u(b):
            t = raw.tile([P, CH, T, COL], BF16, name="u_raw", tag="u_raw", bufs=4, align_bytes=ALIGN)
            nc.sync.dma_start(out=t[:], in_=u[b].rearrange("c (p t) n -> p c t n", t=T))
            st[b]["u_raw"] = t

        def widen(b, c, t, eng):
            if t == 0:
                st[b]["w_pl", c] = work.tile([P, T, DIM], BF16, name="w_pl", tag="w_pl", bufs=4, align_bytes=ALIGN)
            src = st[b]["w_raw", c][:, t, :].bitcast(FP8)
            dst = st[b]["w_pl", c][:, t, :]
            if eng == "s":
                nc.scalar.activation(out=dst, in_=src, func=COPY, scale=wsc[:, t : t + 1])
            else:
                nc.vector.tensor_scalar(out=dst, in0=src, scalar1=wsc[:, t : t + 1], scalar2=None, op0=MULT)

        def grouped(b, key):
            tag = "grp_k0" if key == "k0" else "grp"
            st[b]["grp", key] = work.tile([P, DIM * T], BF16, name=tag, tag=tag, bufs=3, align_bytes=ALIGN)
            return st[b]["grp", key]

        def interleave_perm(b, key, planes, eng="v"):
            out = grouped(b, key)
            (nc.vector.tensor_copy if eng == "v" else nc.scalar.copy)(
                out=out[:].rearrange("p (s m t) -> p m t s", s=T, t=T),
                in_=planes[:].rearrange("p t (m s) -> p m t s", s=T),
            )

        def interleave_nat(dst, planes, eng):
            (nc.vector.tensor_copy if eng == "v" else nc.scalar.copy)(
                out=dst.rearrange("p (c i t) -> p c t i", i=4, t=T),
                in_=planes.rearrange("p t (c i) -> p c t i", i=4),
            )

        def interleave_u(b, pe):
            out = work.tile([P, CH * COL * T], BF16, name="grp_u", tag="grp_u", bufs=3, align_bytes=ALIGN)
            st[b]["grp", "u"] = out
            if not pe:
                nc.vector.tensor_copy(
                    out=out[:].rearrange("p (c n i t) -> p c n t i", c=CH, i=4, t=T),
                    in_=st[b]["u_raw"][:].rearrange("p c t (n i) -> p c n t i", i=4),
                )
                return
            bk = bank([P, 1024], BF16, "u_bank")
            for c in range(CH):
                nc.tensor.matmul(
                    out=bk[:, c * 512 : (c + 1) * 512].rearrange("p (n t) -> p n t", t=T),
                    lhsT=ident_bf[:], rhs=st[b]["u_raw"][:, c].rearrange("p t n -> p n t"), start=True, stop=True,
                )
            nc.scalar.copy(out=out[:], in_=bk[:])

        def pe_interleave(b, key, planes):
            view = planes[:].rearrange("p t (m s) -> p s m t", s=T)
            out = grouped(b, key)
            st[b]["ilb", key] = []
            for h in range(2):
                bk = bank([P, 1024], BF16, "il_bank")
                for j in range(2):
                    nc.tensor.matmul(
                        out=bk[:, j * 512 : (j + 1) * 512].rearrange("p (m t) -> p m t", t=T),
                        lhsT=ident_bf[:], rhs=view[:, 2 * h + j], start=True, stop=True,
                    )
                st[b]["ilb", key].append(bk)

        def pe_interleave_out(b, key, h):
            nc.scalar.copy(out=st[b]["grp", key][:, h * 1024 : (h + 1) * 1024], in_=st[b]["ilb", key][h][:])

        def quantize(b, key, width, lo=0, hi=None):
            if lo > 0:
                q, s = st[b]["q", key]
                nc.vector.quantize_mx(
                    out=q[:, lo:width].bitcast(FP8X4), scales=s[:, lo:width], in_=st[b]["grp", key][:, lo * T : width * T]
                )
                return
            hi = hi or width
            q = quant.tile([P, width], U32, name="q_" + key, tag="q_" + key, bufs=2, align_bytes=ALIGN)
            s = quant.tile([P, width], U8, name="s_" + key, tag="s_" + key, bufs=2, align_bytes=ALIGN)
            nc.vector.quantize_mx(out=q[:, 0:hi].bitcast(FP8X4), scales=s[:, 0:hi], in_=st[b]["grp", key][:, 0 : hi * T])
            st[b]["q", key] = (q, s)

        def mx(out, lhs, lc, rhs, rc, start=True, stop=True):
            lq, ls = lhs
            rq, rs = rhs
            nc.tensor.matmul_mx(
                out=out, lhsT=lq[:, lc].bitcast(FP8X4), lhsT_scale=ls[:, lc],
                rhs=rq[:, rc].bitcast(FP8X4), rhs_scale=rs[:, rc], start=start, stop=stop,
            )

        def blk(i):
            return slice(i * P, (i + 1) * P)

        ALLC = slice(0, DIM)

        def map_x(b, c):
            lhs, rhs = (st[b]["q", "k0"], st[b]["q", "w0"]) if c == 0 else (st[b]["q", "w1"], st[b]["q", "k1"])
            bk = bank([P, T, P], F32, "x_bank")
            for t in range(T):
                mx(bk[:, t, :], lhs, blk(t), rhs, blk(t))
            st[b]["x", c] = bk

        def map_t(b, c, t):
            lhs, rhs = (st[b]["q", "k0"], st[b]["q", "w0"]) if c == 0 else (st[b]["q", "w1"], st[b]["q", "k1"])
            bk = bank([P, DIM], F32, "m_bank")
            mx(bk[:], lhs, blk(t), rhs, ALLC)
            if t == 0:
                st[b]["pl", c] = work.tile([P, T, DIM], BF16, name="m_pl", tag="m_pl", bufs=3, align_bytes=ALIGN)
            st[b]["mb", c, t] = bk

        def map_h(b):
            bk = bank([P, T, COL], F32, "h_bank")
            for t in range(T):
                mx(bk[:, t, :], st[b]["q", "k0"], blk(t), st[b]["q", "u"], blk(0))
            st[b]["hb"] = bk

        def plane_out(b, c, t, eng="s"):
            for lo, hi in ((0, t * P), ((t + 1) * P, DIM)):
                if hi > lo:
                    dst = st[b]["pl", c][:, t, lo:hi]
                    src = st[b]["mb", c, t][:, lo:hi]
                    if eng == "s":
                        nc.scalar.activation(out=dst, in_=src, func=COPY, scale=neg[:, t, c : c + 1])
                    else:
                        nc.vector.tensor_scalar(out=dst, in0=src, scalar1=neg[:, t, c : c + 1], scalar2=None, op0=MULT)

        def diag_out(b, c):
            for t in range(T):
                nc.vector.scalar_tensor_tensor(
                    out=st[b]["pl", c][:, t, blk(t)], in0=st[b]["x", c][:, t, :], scalar=neg[:, t, c : c + 1],
                    in1=st[b]["diag"][:, c * T + t, :], op0=MULT, op1=ADD,
                )

        def h_out(b):
            out = work.tile([P, COL * T], BF16, name="grp_h", tag="grp_h", bufs=2, align_bytes=ALIGN)
            nc.vector.tensor_tensor(
                out=out[:].rearrange("p (n t) -> p n t", t=T),
                in0=st[b]["hb"][:].rearrange("p t n -> p n t"),
                in1=coef[:, :, 16].unsqueeze(1).to_broadcast([P, COL, T]),
                op=MULT,
            )
            st[b]["grp", "h"] = out

        def interleave_m(b, c, lo=0, hi=DIM, eng="v"):
            if lo == 0:
                st[b]["grp", "m%d" % c] = work.tile([P, DIM * T], BF16, name="grp_m", tag="grp_m", bufs=3, align_bytes=ALIGN)
            interleave_nat(st[b]["grp", "m%d" % c][:, lo * T : hi * T], st[b]["pl", c][:, :, lo:hi], eng)

        parks = [mm_out[B - 1 - i].rearrange("d f -> (d f)")[0 : MATS * P * PITCH] for i in range(2)]

        def diag_tile(b):
            st[b]["diag"] = work.tile([P, MATS, P], F32, name="diag", tag="diag", bufs=3, align_bytes=ALIGN)

        def build_diag(b, c):
            for t in range(T):
                i = c * T + t
                nc.scalar.activation(
                    out=st[b]["diag"][:, i, :], in_=ident[:], func=COPY, scale=seed[:, b * MATS + i, 0:1]
                )

        def park_seed(b):
            nc.sync.dma_start(
                out=parks[b % 2].rearrange("(i p w) -> p i w", p=P, w=PITCH)[:, :, 0:SEED],
                in_=seed[:, b * MATS : (b + 1) * MATS, :],
            )

        def load_diag(b):
            diag_tile(b)
            nc.sync.dma_start(
                out=st[b]["diag"][:],
                in_=parks[b % 2].rearrange("(i x) -> i x", i=MATS)[:, 0 : P * (PITCH - 1)].rearrange("i (p w) -> p i w", p=P)[:, :, 0:P],
            )

        def merge(b, s):
            bk = bank([P, DIM], F32, "o_bank")
            mx(bk[:], st[b]["q", "m1"], blk(s), st[b]["q", "m0"], ALLC)
            st[b]["ob", s] = bk

        def merge_h(b, lo=0, hi=T):
            if lo == 0:
                st[b]["ohb"] = bank([P, T, COL], F32, "oh_bank")
            bk = st[b]["ohb"]
            for s in range(lo, hi):
                mx(bk[:, s, :], st[b]["q", "k1"], blk(s), st[b]["q", "u"], blk(1), True, False)
                mx(bk[:, s, :], st[b]["q", "m1"], blk(s), st[b]["q", "h"], blk(0), False, True)

        def merge_out(b, s, eng="s"):
            if s == 0:
                st[b]["o"] = work.tile([P, T, DIM], F32, name="o_sb", tag="o_sb", bufs=2, align_bytes=ALIGN)
            dst = st[b]["o"][:, s, :].rearrange("p (m j) -> p m j", j=T)
            src = st[b]["ob", s][:].rearrange("p (j m) -> p m j", j=T)
            if eng == "s":
                nc.scalar.copy(out=dst, in_=src)
            else:
                nc.vector.tensor_copy(out=dst, in_=src)

        def merge_h_out(b, eng="s"):
            o = work.tile([P, T, COL], F32, name="oh_sb", tag="oh_sb", bufs=2, align_bytes=ALIGN)
            if eng == "s":
                nc.scalar.copy(out=o[:], in_=st[b]["ohb"][:])
            else:
                nc.vector.tensor_copy(out=o[:], in_=st[b]["ohb"][:])
            st[b]["oh"] = o

        def store(b, lo, hi):
            nc.sync.dma_start(out=mm_out[b].rearrange("(m s) f -> m s f", s=T)[:, lo:hi, :], in_=st[b]["o"][:, lo:hi, :])

        def store_h(b):
            nc.sync.dma_start(out=hh_out[b].rearrange("(m s) f -> m s f", s=T), in_=st[b]["oh"][:])

        nc.vector.memset(rows[:], 0.0)
        nc.vector.memset(warm[:], 0.0)
        make_identity(nc, ident_bf[:])
        make_identity(nc, ident[:])
        nc.gpsimd.memset(seed[:], 0.0)
        nc.gpsimd.memset(zeros[:], 0.0)
        nc.scalar.dma_start(out=wsc[:], in_=w_scale.rearrange("a b (p t) o -> p (a b t o)", t=T))
        nc.scalar.dma_start(out=rows[0:16, :], in_=g.rearrange("b c d -> (b c) d"))
        nc.scalar.dma_start(out=rows[16:17, :], in_=gb.unsqueeze(0))
        nc.scalar.dma_start(out=rows[17:18, :], in_=ga.unsqueeze(0))
        nc.scalar.activation(out=warm[:], in_=warm[:], func=COPY)
        load_w(0, 0)
        load_k(0, 0)
        load_u(0)
        load_w(0, 1)
        load_k(0, 1)
        load_w(1, 0)
        load_k(1, 0)
        load_u(1)
        load_w(1, 1)
        load_k(1, 1)
        load_w(2, 0)
        load_k(2, 0)
        load_u(2)
        for park in parks:
            nc.sync.dma_start(out=park.rearrange("(p x) -> p x", p=P), in_=zeros[:])

        for t in range(T):
            widen(0, 0, t, "s" if t == 0 else "v")
        pe_interleave(0, "k0", st[0]["k_raw", 0])
        interleave_perm(0, "w0", st[0]["w_pl", 0])
        tb = bank([P, T, P], BF16, "t_bank")
        for t in range(T):
            nc.tensor.transpose(tb[:, t, :], rows[:].rearrange("r (m t) -> r t m", t=T)[:, t, :], ident_bf[:])
        pe_interleave_out(0, "k0", 0)
        pe_interleave_out(0, "k0", 1)
        interleave_u(0, False)
        quantize(0, "w0", DIM)
        interleave_perm(0, "k1", st[0]["k_raw", 1])
        quantize(0, "k0", DIM)
        nc.vector.tensor_copy(out=coef[:], in_=tb[:, :, 0:18])
        nc.vector.tensor_scalar(out=neg[:], in0=coef[:, :, 16:18], scalar1=-1.0, scalar2=None, op0=MULT)
        quantize(0, "u", CH * COL)
        nc.vector.tensor_tensor(
            out=seed[:, :, 0].rearrange("p (b c t) -> p t b c", c=CH, t=T),
            in0=coef[:, :, 0:16].rearrange("p t (b c) -> p t b c", c=CH),
            in1=coef[:, :, 16:18].unsqueeze(2).to_broadcast([P, T, B, CH]),
            op=MULT,
        )
        for t in range(T):
            widen(0, 1, t, "s")
        diag_tile(0)
        build_diag(0, 0)
        V_PLANES = [(b, 1, 3) for b in range(2, B)] + [(1, 0, 2), (1, 0, 3), (2, 0, 1), (2, 0, 2)]

        def widen_all(b, c):
            for t in range(T):
                widen(b, c, t, "v" if (b, c, t) in V_PLANES else "s")

        def lead_inputs(b):
            interleave_u(b, True)
            pe_interleave(b, "k0", st[b]["k_raw", 0])
            pe_interleave_out(b, "k0", 0)
            pe_interleave_out(b, "k0", 1)

        map_x(0, 0)
        for t in range(T):
            map_t(0, 0, t)
        map_h(0)
        for t in range(T):
            plane_out(0, 0, t)
        interleave_perm(0, "w1", st[0]["w_pl", 1])
        build_diag(0, 1)
        diag_out(0, 0)
        quantize(0, "k1", DIM)
        h_out(0)
        quantize(0, "w1", DIM)
        widen_all(1, 0)
        lead_inputs(1)

        for b in range(B):
            n = b + 1
            nx = n < B
            lead = b + 2 < B
            first = b == 0
            if first:
                park_seed(1)
                park_seed(2)
            if lead:
                load_w(b + 2, 1)
                load_k(b + 2, 1)
            if b + 3 < B:
                load_w(b + 3, 0)
                load_k(b + 3, 0)
                load_u(b + 3)
            if first:
                load_diag(1)
            if lead:
                load_diag(b + 2)
            if b + 3 < B:
                park_seed(b + 3)
            early = 2 if not nx else 0 if first else T
            for s in range(early):
                merge(b - 1, s)
            if nx and not first:
                merge_h(b - 1)
            map_x(b, 1)
            for t in range(T):
                map_t(b, 1, t)
            for s in range(early):
                merge_out(b - 1, s)
                if s % 2 == 1:
                    store(b - 1, s - 1, s + 1)
            if not nx:
                for t in range(T):
                    plane_out(b, 1, t)
                for s in range(early, T):
                    merge(b - 1, s)
                merge_h(b - 1)
                for s in range(early, T):
                    merge_out(b - 1, s)
                store(b - 1, early, T)
            if not first:
                merge_h_out(b - 1)
                store_h(b - 1)
            if nx:
                for t in range(T):
                    plane_out(b, 1, t)
                if first:
                    interleave_perm(n, "k1", st[n]["k_raw", 1])
                else:
                    interleave_perm(n, "w0", st[n]["w_pl", 0])
                diag_out(b, 1)
                interleave_m(b, 0)
                quantize(n, "k1" if first else "w0", DIM)
                quantize(b, "m0", DIM)
                widen_all(n, 1)
                if first:
                    interleave_perm(n, "w0", st[n]["w_pl", 0])
                else:
                    interleave_perm(n, "k1", st[n]["k_raw", 1], "s" if n == B - 1 else "v")
                quantize(n, "k0", DIM)
                if first:
                    quantize(n, "w0", DIM)
                quantize(n, "u", CH * COL)
                quantize(b, "h", COL)
                if lead:
                    lead_inputs(b + 2)
                interleave_m(b, 1)
                if lead and not first:
                    quantize(n, "k1", DIM)
                interleave_perm(n, "w1", st[n]["w_pl", 1])
                if lead:
                    widen_all(b + 2, 0)
                quantize(b, "m1", DIM)
                if not lead:
                    quantize(n, "k1", DIM)
                map_x(n, 0)
                for t in range(T):
                    map_t(n, 0, t)
                map_h(n)
                for t in range(T):
                    plane_out(n, 0, t)
                quantize(n, "w1", DIM)
                diag_out(n, 0)
                h_out(n)
            else:
                interleave_m(b, 0)
                diag_out(b, 1)
                quantize(b, "m0", DIM)
                interleave_m(b, 1, 0, 256)
                quantize(b, "h", COL)
                quantize(b, "m1", DIM, 0, 256)
                interleave_m(b, 1, 256, DIM)
                quantize(b, "m1", DIM, 256)
                for s in range(T):
                    merge(b, s)
                    if s % 2 == 1:
                        merge_h(b, s - 1, s + 1)
                    merge_out(b, s, "v" if s % 2 else "s")
                    store(b, s, s + 1)
                merge_h_out(b)
                store_h(b)
